import numpy as np
import ml_dtypes


def mxq(x, axis, fmt="e4m3"):
    dtype, down = {"e4m3": (ml_dtypes.float8_e4m3fn, 7), "e5m2": (ml_dtypes.float8_e5m2, 14)}[fmt]
    v = np.moveaxis(np.asarray(x, np.float32).astype(ml_dtypes.bfloat16).astype(np.float64), axis, -1)
    blocks = v.reshape(v.shape[:-1] + (-1, 32))
    amax = np.abs(blocks).max(-1, keepdims=True)
    byte = np.maximum(np.where(amax > 0, np.frexp(amax)[1] - 1 + 127, 0) - down, 1)
    scale = np.exp2(byte - 127.0)
    codes = (blocks / scale).astype(np.float32).astype(dtype).astype(np.float64)
    return np.moveaxis((codes * scale).reshape(v.shape), -1, axis)


WIDE = False


def mx_kscale(k):
    if not WIDE:
        return np.ones(k)
    levels = np.array([10, -10, 5, -5, 0])
    if k % 512:
        return np.exp2(np.random.permutation(np.resize(levels, k // 32))).repeat(32)
    a = np.empty((k // 512, 16))
    for p in range(k // 512):
        a[p, :8] = np.random.permutation(np.resize(levels, 8))
        for g in range(8):
            far = levels[np.abs(levels - a[p, g]) >= 10]
            a[p, g + 8] = far[np.random.randint(len(far))]
    return np.exp2(a.ravel()).repeat(32)


BF16 = ml_dtypes.bfloat16


def bf(x):
    return np.asarray(x, np.float32).astype(BF16)


def f64(x):
    return np.asarray(x).astype(np.float64)


E2M1 = np.array([0.0, 0.5, 1.0, 1.5, 2.0, 3.0, 4.0, 6.0, -0.0, -0.5, -1.0, -1.5, -2.0, -3.0, -4.0, -6.0])


def pack_weight(w, fmt):
    k, n = w.shape
    w = f64(bf(w)).reshape(k // 32, 32, n)
    amax = np.abs(w).max(1)
    if fmt == "e4m3":
        byte = np.frexp(amax)[1] - 1 + 127 - 7
    else:
        mant, ex = np.frexp(amax / 6.0)
        byte = np.where(mant > 0.5, ex, ex - 1) + 127
    byte = np.clip(np.where(amax > 0, byte, 1), 1, 254)
    scaled = (w * np.exp2(127.0 - byte)[:, None, :]).reshape(k, n).astype(np.float32)
    by_word = np.ascontiguousarray(scaled.reshape(k // 512, 128, 4, n).transpose(0, 1, 3, 2))
    if fmt == "e4m3":
        words = by_word.astype(ml_dtypes.float8_e4m3fn).view(np.uint8)
    else:
        c = by_word.astype(ml_dtypes.float4_e2m1fn).view(np.uint8) & 0xF
        words = c[..., 0::2] | (c[..., 1::2] << 4)
    return np.ascontiguousarray(words), np.ascontiguousarray(byte.astype(np.uint8).reshape(k // 512, 16, n))


def unpack_weight(words, scales, fmt):
    g, p, n, _ = words.shape
    if fmt == "e4m3":
        vals = np.ascontiguousarray(words).view(ml_dtypes.float8_e4m3fn).astype(np.float64)
    else:
        nib = np.empty((g, p, n, 4), np.uint8)
        nib[..., 0::2] = words & 0xF
        nib[..., 1::2] = words >> 4
        vals = E2M1[nib]
    vals = vals * np.repeat(np.exp2(scales.astype(np.float64) - 127.0), 8, axis=1)[..., None]
    return vals.transpose(0, 1, 3, 2).reshape(g * 512, n)
def pack4(w):
    words, scales = pack_weight(w, "e2m1")
    return words.reshape(words.shape[0], 128, -1), scales


def unpack4(words, scales):
    return unpack_weight(words.reshape(words.shape[0], 128, -1, 2), scales, "e2m1")


M, D = 512, 1536


def setup_inputs():
    s = mx_kscale(D)
    turn = s[None, :] / s[:, None]
    x = bf(np.random.standard_normal((M, D)) * s)
    w1 = 0.5 * np.random.standard_normal((D, D)) / np.sqrt(D) * turn
    w2 = 0.5 * np.random.standard_normal((D, D)) / np.sqrt(D) * turn
    w3 = 0.35 * np.random.standard_normal((D, D)) / np.sqrt(D) * turn
    w1_words, w1_scales = pack4(w1)
    w2_words, w2_scales = pack4(w2)
    w3_words, w3_scales = pack4(w3)
    c = bf((1 + 0.1 * np.random.standard_normal(D)) / s)
    return {"x": x,
            "w1_words": w1_words, "w1_scales": w1_scales,
            "w2_words": w2_words, "w2_scales": w2_scales,
            "w3_words": w3_words, "w3_scales": w3_scales,
            "c": c}


def reference(x, w1_words, w1_scales, w2_words, w2_scales, w3_words, w3_scales, c):
    x = f64(x)
    w1 = unpack4(w1_words, w1_scales)
    w2 = unpack4(w2_words, w2_scales)
    w3 = unpack4(w3_words, w3_scales)
    h1 = x + np.maximum(mxq(x, 1, "e4m3") @ w1, 0.0)
    h2 = h1 + np.maximum(mxq(h1, 1, "e4m3") @ w2, 0.0)
    return (h2 + (mxq(h2, 1, "e4m3") @ w3)) * f64(c)

@@ -1,0 +1,256 @@
+from contextlib import ExitStack
+
+import concourse.mybir as mybir
+from concourse.masks import make_identity
+
+M, D = 512, 1536
+FLOPS = 3 * 2 * M * D * D
+
+F32 = mybir.dt.float32
+BF16 = mybir.dt.bfloat16
+I32 = mybir.dt.int32
+U32 = mybir.dt.uint32
+U8 = mybir.dt.uint8
+FP8X4 = mybir.dt.float8_e4m3fn_x4
+FP4X4 = mybir.dt.float4_e2m1fn_x4
+ALU = mybir.AluOpType
+
+P = 128
+KP = 512
+G = D // KP
+NB = 512
+TILES = M // P
+BANKS = 8
+
+
+def tile_three_residual_adapters_t2_kernel(
+    tc, x, w1_words, w1_scales, w2_words, w2_scales, w3_words, w3_scales, c, out
+):
+    nc = tc.nc
+    with ExitStack() as ctx:
+        sb = ctx.enter_context(tc.tile_pool(name="sb", bufs=1))
+        ps = ctx.enter_context(tc.psum_pool(name="ps", bufs=1))
+        ctx.enter_context(tc.manual_schedule())
+
+        used = []
+
+        def new_bank():
+            n = len(used)
+            used.append(n)
+            return ps.tile([P, NB], F32, name="ps%d" % n, tag="bank%d" % (n % BANKS))
+
+        words_in = [w1_words, w2_words, w3_words]
+        scales_in = [w1_scales, w2_scales, w3_scales]
+        planes = [sb.tile([P, G * D], U8, name="plane%d" % s, align_bytes=64) for s in range(3)]
+        for s in range(3):
+            nc.vector.memset(planes[s][:].bitcast(I32), 0)
+        ident = sb.tile([P, P], F32, name="ident")
+        make_identity(nc, ident[:])
+
+        xs = [sb.tile([P, D], BF16, name="x%d" % t, align_bytes=64) for t in range(TILES)]
+        w1 = [sb.tile([P, 2 * D], U8, name="w1_%d" % g, align_bytes=64) for g in range(G)]
+        w2 = sb.tile([P, G * 2 * D], U8, name="w2", align_bytes=64)
+        w3 = sb.tile([P, G * 2 * D], U8, name="w3", align_bytes=64)
+        cb = sb.tile([P, D], BF16, name="cb")
+
+        def load_x(t):
+            nc.sync.dma_start(out=xs[t][:], in_=x[t * P : (t + 1) * P, :])
+
+        def load_scales(s):
+            src = scales_in[s].bitcast(I32).rearrange("g (q r) n -> r q g n", r=4)
+            dst = planes[s][:].bitcast(I32)
+            for r in range(4):
+                nc.sync.dma_start(out=dst[r:P:32, :].rearrange("q (g n) -> q g n", g=G), in_=src[r])
+
+        def load_w1(g):
+            nc.sync.dma_start(out=w1[g][:].bitcast(I32), in_=w1_words[g].bitcast(I32))
+
+        def load_w(s, tile):
+            nc.sync.dma_start(
+                out=tile[:].bitcast(I32).rearrange("p (g n) -> p g n", g=G),
+                in_=words_in[s].bitcast(I32).rearrange("g p n -> p g n"),
+            )
+
+        load_x(0)
+        load_scales(0)
+        load_w1(0)
+        load_x(1)
+        load_w1(1)
+        load_w1(2)
+        load_x(2)
+        load_x(3)
+        load_scales(1)
+        load_w(1, w2)
+        load_scales(2)
+        load_w(2, w3)
+        nc.sync.dma_start(out=cb[:], in_=c.partition_broadcast(P))
+
+        def weight(s, g, j):
+            if s == 0:
+                wb = w1[g][:, 2 * NB * j : 2 * NB * (j + 1)]
+            else:
+                wb = (w2 if s == 1 else w3)[:, 2 * D * g + 2 * NB * j : 2 * D * g + 2 * NB * (j + 1)]
+            return wb.bitcast(FP4X4), planes[s][:, D * g + NB * j : D * g + NB * (j + 1)]
+
+        halves = {}
+        quantised = {}
+        resid = {}
+        for t in range(TILES):
+            for j in range(G):
+                resid[(0, t, j)] = xs[t][:, NB * j : NB * (j + 1)]
+
+        def x_direct(t):
+            w = xs[t][:].bitcast(F32)
+            for g in range(G):
+                halves[(0, t, g)] = [w[:, 256 * g + u : 256 * (g + 1) : 2] for u in range(2)]
+
+        def x_sorted(t):
+            srt = sb.tile([P, D // 2], F32, name="xsort%d" % t)
+            nc.vector.tensor_copy(
+                out=srt[:].rearrange("p (g u m) -> p g u m", g=G, u=2),
+                in_=xs[t][:].bitcast(F32).rearrange("p (g m u) -> p g u m", g=G, u=2),
+            )
+            for g in range(G):
+                halves[(0, t, g)] = [srt[:, 256 * g + P * u : 256 * g + P * (u + 1)] for u in range(2)]
+
+        def turn(chunks):
+            done = []
+            for keys in chunks:
+                bank = new_bank()
+                for i, key in enumerate(keys):
+                    for u in range(2):
+                        nc.tensor.transpose(bank[:, (2 * i + u) * P : (2 * i + u + 1) * P], halves[key][u], ident[:])
+                done.append((keys, bank))
+            return done
+
+        def copy_out(item):
+            keys, bank = item
+            n = len(keys)
+            label = "%d%d%d" % keys[0]
+            grp = sb.tile([P, n * KP], BF16, name="grp" + label, align_bytes=64)
+            nc.scalar.copy(
+                out=grp[:].bitcast(F32).rearrange("p (i r u) -> p i r u", i=n, u=2),
+                in_=bank[:, : n * 2 * P].rearrange("p (i u r) -> p i r u", i=n, u=2),
+            )
+            return keys, grp
+
+        def quantise(item):
+            keys, grp = item
+            n = len(keys)
+            label = "%d%d%d" % keys[0]
+            codes = sb.tile([P, n * P], U32, name="codes" + label, align_bytes=64)
+            scl = sb.tile([P, n * P], U8, name="scl" + label, align_bytes=64)
+            nc.vector.quantize_mx(out=codes[:].bitcast(FP8X4), scales=scl[:], in_=grp[:])
+            for i, key in enumerate(keys):
+                quantised[key] = (codes[:, i * P : (i + 1) * P], scl[:, i * P : (i + 1) * P])
+
+        def mm(acc, s, t, g, j):
+            codes, scl = quantised[(s, t, g)]
+            wb, ws = weight(s, g, j)
+            nc.tensor.matmul_mx(
+                out=acc[:], lhsT=codes.bitcast(FP8X4), lhsT_scale=scl, rhs=wb, rhs_scale=ws,
+                start=(g == 0), stop=(g == G - 1),
+            )
+
+        def column(s, t, j):
+            acc = new_bank()
+            for g in range(G):
+                mm(acc, s, t, g, j)
+            return acc
+
+        def add_relu(acc, s, t, j):
+            h = sb.tile([P, NB], F32, name="h%d%d%d" % (s + 1, t, j))
+            nc.vector.scalar_tensor_tensor(
+                out=h[:], in0=acc[:], scalar=0.0, in1=resid[(s, t, j)], op0=ALU.max, op1=ALU.add
+            )
+            resid[(s + 1, t, j)] = h[:]
+
+        def cast(s, t, j):
+            hb = sb.tile([P, NB], BF16, name="hb%d%d%d" % (s + 1, t, j))
+            nc.scalar.copy(
+                out=hb[:].rearrange("p (u m e) -> p u m e", u=2, e=2),
+                in_=resid[(s + 1, t, j)].rearrange("p (m u e) -> p u m e", u=2, e=2),
+            )
+            w = hb[:].bitcast(F32)
+            halves[(s + 1, t, j)] = [w[:, P * u : P * (u + 1)] for u in range(2)]
+
+        def add_last(acc, t, j):
+            nc.vector.tensor_tensor(out=resid[(1, t, j)], in0=acc[:], in1=resid[(2, t, j)], op=ALU.add)
+
+        def scale_store(engine, t, j):
+            engine.tensor_tensor(
+                out=resid[(2, t, j)], in0=resid[(1, t, j)], in1=cb[:, NB * j : NB * (j + 1)], op=ALU.mult
+            )
+            nc.sync.dma_start(out=out[t * P : (t + 1) * P, NB * j : NB * (j + 1)], in_=resid[(2, t, j)])
+
+        def groups(s, t):
+            return [(s, t, g) for g in range(G)]
+
+        def in_twos(keys):
+            return [keys[i : i + 2] for i in range(0, len(keys), 2)]
+
+        x_direct(0)
+        x_direct(1)
+        k0 = groups(0, 0)
+        for item in [copy_out(i) for i in turn([k0[:1], k0[1:]])]:
+            quantise(item)
+        accs = [new_bank() for j in range(G)]
+        for j in range(G):
+            mm(accs[j], 0, 0, 0, j)
+        for item in [copy_out(i) for i in turn(in_twos(groups(0, 1)))]:
+            quantise(item)
+        x_sorted(2)
+        for g in range(1, G):
+            for j in range(G):
+                mm(accs[j], 0, 0, g, j)
+        turned = turn(in_twos(groups(0, 2)))
+        for j in range(G):
+            add_relu(accs[j], 0, 0, j)
+        first = copy_out(turned[0])
+        cast(0, 0, 0)
+        second = copy_out(turned[1])
+        cast(0, 0, 1)
+        cast(0, 0, 2)
+        x_sorted(3)
+
+        units = [(0, 1), (0, 2), (0, 3), (1, 0), (1, 1), (1, 2), (2, 0), (1, 3), (2, 1), (2, 2), (2, 3)]
+        runs = {
+            (0, 1): [(0, 3), (1, 0)],
+            (0, 3): [(1, 1), (1, 2)],
+            (1, 1): [(1, 3), (2, 0)],
+            (2, 0): [(2, 1), (2, 2)],
+            (2, 1): [(2, 3)],
+        }
+        on_pool = {(0, 0), (0, 1), (0, 2), (1, 0), (1, 2), (2, 1), (3, 0)}
+        to_quantise = [first, second]
+        late_mult = []
+        for s, t in units:
+            for j in range(G):
+                acc = column(s, t, j)
+                if s < 2:
+                    add_relu(acc, s, t, j)
+                else:
+                    add_last(acc, t, j)
+                    for tj in late_mult:
+                        scale_store(nc.vector, *tj)
+                    late_mult = []
+                    if (t, j) in on_pool:
+                        scale_store(nc.gpsimd, t, j)
+                    else:
+                        late_mult = [(t, j)]
+                if j == 0:
+                    for item in to_quantise:
+                        quantise(item)
+                    to_quantise = []
+                if s < 2 and (j < G - 1 or (s, t) not in runs):
+                    cast(s, t, j)
+            if (s, t) in runs:
+                keys = [k for st in runs[(s, t)] for k in groups(*st)]
+                items = [copy_out(i) for i in turn(in_twos(keys))]
+                if s < 2:
+                    cast(s, t, G - 1)
+                for item in items[:2]:
+                    quantise(item)
+                to_quantise = items[2:]
+        for tj in late_mult:
+            scale_store(nc.vector, *tj)

@@ -33,11 +33,15 @@ def tile_three_residual_adapters_t2_kernel(
         ctx.enter_context(tc.manual_schedule())
 
         used = []
+        ring = list(range(BANKS))
 
-        def new_bank():
+        def new_bank(keep=False, back=None):
             n = len(used)
             used.append(n)
-            return ps.tile([P, NB], F32, name="ps%d" % n, tag="bank%d" % (n % BANKS))
+            b = ring.pop(0 if back is None else BANKS - back)
+            if not keep:
+                ring.append(b)
+            return ps.tile([P, NB], F32, name="ps%d" % n, tag="bank%d" % b)
 
         words_in = [w1_words, w2_words, w3_words]
         scales_in = [w1_scales, w2_scales, w3_scales]
@@ -51,16 +55,19 @@ def tile_three_residual_adapters_t2_kernel(
         w1 = [sb.tile([P, 2 * D], U8, name="w1_%d" % g, align_bytes=64) for g in range(G)]
         w2 = sb.tile([P, G * 2 * D], U8, name="w2", align_bytes=64)
         w3 = sb.tile([P, G * 2 * D], U8, name="w3", align_bytes=64)
-        cb = sb.tile([P, D], BF16, name="cb")
+        cb = sb.tile([P, 2 * NB], BF16, name="cb")
 
         def load_x(t):
             nc.sync.dma_start(out=xs[t][:], in_=x[t * P : (t + 1) * P, :])
 
-        def load_scales(s):
+        def load_scales(s, g0, g1):
             src = scales_in[s].bitcast(I32).rearrange("g (q r) n -> r q g n", r=4)
             dst = planes[s][:].bitcast(I32)
             for r in range(4):
-                nc.sync.dma_start(out=dst[r:P:32, :].rearrange("q (g n) -> q g n", g=G), in_=src[r])
+                nc.sync.dma_start(
+                    out=dst[r:P:32, g0 * D // 4 : g1 * D // 4].rearrange("q (g n) -> q g n", g=g1 - g0),
+                    in_=src[r][:, g0:g1, :],
+                )
 
         def load_w1(g):
             nc.sync.dma_start(out=w1[g][:].bitcast(I32), in_=w1_words[g].bitcast(I32))
@@ -72,18 +79,22 @@ def tile_three_residual_adapters_t2_kernel(
             )
 
         load_x(0)
-        load_scales(0)
-        load_w1(0)
         load_x(1)
+        load_scales(0, 0, 1)
+        load_w1(0)
+        load_scales(0, 1, G)
         load_w1(1)
         load_w1(2)
         load_x(2)
         load_x(3)
-        load_scales(1)
+        load_scales(1, 0, G)
         load_w(1, w2)
-        load_scales(2)
+        load_scales(2, 0, G)
         load_w(2, w3)
-        nc.sync.dma_start(out=cb[:], in_=c.partition_broadcast(P))
+        c_col = sb.tile([P, 2], F32, name="c_col")
+        with nc.allow_non_contiguous_dma(reason="one word of c to a partition"):
+            nc.sync.dma_start(out=c_col[:], in_=c[2 * NB :].bitcast(F32).rearrange("(i p) -> p i", p=P))
+        nc.sync.dma_start(out=cb[:], in_=c[: 2 * NB].partition_broadcast(P))
 
         def weight(s, g, j):
             if s == 0:
@@ -113,10 +124,10 @@ def tile_three_residual_adapters_t2_kernel(
             for g in range(G):
                 halves[(0, t, g)] = [srt[:, 256 * g + P * u : 256 * g + P * (u + 1)] for u in range(2)]
 
-        def turn(chunks):
+        def turn(chunks, back=None):
             done = []
             for keys in chunks:
-                bank = new_bank()
+                bank = new_bank(back=back)
                 for i, key in enumerate(keys):
                     for u in range(2):
                         nc.tensor.transpose(bank[:, (2 * i + u) * P : (2 * i + u + 1) * P], halves[key][u], ident[:])
@@ -177,11 +188,22 @@ def tile_three_residual_adapters_t2_kernel(
         def add_last(acc, t, j):
             nc.vector.tensor_tensor(out=resid[(1, t, j)], in0=acc[:], in1=resid[(2, t, j)], op=ALU.add)
 
-        def scale_store(engine, t, j):
-            engine.tensor_tensor(
-                out=resid[(2, t, j)], in0=resid[(1, t, j)], in1=cb[:, NB * j : NB * (j + 1)], op=ALU.mult
-            )
+        def scale_store(t, j):
+            if j < G - 1:
+                nc.gpsimd.tensor_tensor(
+                    out=resid[(2, t, j)], in0=resid[(1, t, j)], in1=cb[:, NB * j : NB * (j + 1)], op=ALU.mult
+                )
+            else:
+                nc.vector.tensor_tensor(out=resid[(2, t, j)], in0=resid[(1, t, j)], in1=c_last[0], op=ALU.mult)
             nc.sync.dma_start(out=out[t * P : (t + 1) * P, NB * j : NB * (j + 1)], in_=resid[(2, t, j)])
+
+        c_last = []
+
+        def spread_c():
+            bank = new_bank(keep=True)
+            for i in range(2):
+                nc.tensor.transpose(bank[:, i * P : (i + 1) * P], c_col[:, i : i + 1].to_broadcast([P, P]), ident[:])
+            c_last.append(bank[:, : 2 * P].bitcast(BF16))
 
         def groups(s, t):
             return [(s, t, g) for g in range(G)]
@@ -191,38 +213,44 @@ def tile_three_residual_adapters_t2_kernel(
 
         x_direct(0)
         x_direct(1)
-        k0 = groups(0, 0)
-        for item in [copy_out(i) for i in turn([k0[:1], k0[1:]])]:
-            quantise(item)
-        accs = [new_bank() for j in range(G)]
-        for j in range(G):
-            mm(accs[j], 0, 0, 0, j)
-        for item in [copy_out(i) for i in turn(in_twos(groups(0, 1)))]:
-            quantise(item)
+        for t in range(2):
+            for item in [copy_out(i) for i in turn(in_twos(groups(0, t)))]:
+                quantise(item)
         x_sorted(2)
-        for g in range(1, G):
-            for j in range(G):
-                mm(accs[j], 0, 0, g, j)
-        turned = turn(in_twos(groups(0, 2)))
-        for j in range(G):
-            add_relu(accs[j], 0, 0, j)
-        first = copy_out(turned[0])
-        cast(0, 0, 0)
-        second = copy_out(turned[1])
-        cast(0, 0, 1)
-        cast(0, 0, 2)
         x_sorted(3)
+        accs = {}
+        for t in range(2):
+            for j in range(G):
+                accs[(t, j)] = new_bank()
+        for g in range(G - 1):
+            for t in range(2):
+                for j in range(G):
+                    mm(accs[(t, j)], 0, t, g, j)
+        x2 = [copy_out(i) for i in turn(in_twos(groups(0, 2)))]
+        for t in range(2):
+            for j in range(G):
+                mm(accs[(t, j)], 0, t, G - 1, j)
+        turned = turn(in_twos(groups(0, 3)), back=2)
+        for j in range(2):
+            add_relu(accs[(0, j)], 0, 0, j)
+            cast(0, 0, j)
+        for item in x2:
+            quantise(item)
+        x3 = [copy_out(i) for i in turned]
+        for t, j in [(0, 2), (1, 0), (1, 1), (1, 2)]:
+            add_relu(accs[(t, j)], 0, t, j)
+            cast(0, t, j)
 
-        units = [(0, 1), (0, 2), (0, 3), (1, 0), (1, 1), (1, 2), (2, 0), (1, 3), (2, 1), (2, 2), (2, 3)]
+        units = [(0, 2), (0, 3), (1, 0), (1, 1), (1, 2), (2, 0), (1, 3), (2, 1), (2, 2), (2, 3)]
         runs = {
-            (0, 1): [(0, 3), (1, 0)],
-            (0, 3): [(1, 1), (1, 2)],
-            (1, 1): [(1, 3), (2, 0)],
+            (0, 2): [(1, 0), (1, 1)],
+            (1, 0): [(1, 2), (1, 3)],
+            (1, 1): [(2, 0)],
             (2, 0): [(2, 1), (2, 2)],
             (2, 1): [(2, 3)],
         }
-        on_pool = {(0, 0), (0, 1), (0, 2), (1, 0), (1, 2), (2, 1), (3, 0)}
-        to_quantise = [first, second]
+        to_quantise = x3
+        late_cast = []
         late_mult = []
         for s, t in units:
             for j in range(G):
@@ -231,26 +259,37 @@ def tile_three_residual_adapters_t2_kernel(
                     add_relu(acc, s, t, j)
                 else:
                     add_last(acc, t, j)
-                    for tj in late_mult:
-                        scale_store(nc.vector, *tj)
-                    late_mult = []
-                    if (t, j) in on_pool:
-                        scale_store(nc.gpsimd, t, j)
-                    else:
-                        late_mult = [(t, j)]
                 if j == 0:
+                    for tj in late_mult:
+                        scale_store(*tj)
+                    late_mult = []
                     for item in to_quantise:
                         quantise(item)
                     to_quantise = []
-                if s < 2 and (j < G - 1 or (s, t) not in runs):
-                    cast(s, t, j)
+                if s == 2 and j < G - 1:
+                    scale_store(t, j)
+                if s < 2:
+                    late_cast.append((s, t, j))
+                    if j < G - 1 or (s, t) not in runs:
+                        for stj in late_cast:
+                            cast(*stj)
+                        late_cast = []
+            if s == 2:
+                late_mult = [(t, G - 1)]
             if (s, t) in runs:
                 keys = [k for st in runs[(s, t)] for k in groups(*st)]
-                items = [copy_out(i) for i in turn(in_twos(keys))]
-                if s < 2:
-                    cast(s, t, G - 1)
+                turned = turn(in_twos(keys))
+                if (s, t) == (1, 1):
+                    spread_c()
+                items = [copy_out(i) for i in turned]
+                for stj in late_cast:
+                    cast(*stj)
+                late_cast = []
+                for tj in late_mult:
+                    scale_store(*tj)
+                late_mult = []
                 for item in items[:2]:
                     quantise(item)
                 to_quantise = items[2:]
         for tj in late_mult:
-            scale_store(nc.vector, *tj)
+            scale_store(*tj)

@@ -55,7 +55,8 @@ def tile_three_residual_adapters_t2_kernel(
         w1 = [sb.tile([P, 2 * D], U8, name="w1_%d" % g, align_bytes=64) for g in range(G)]
         w2 = sb.tile([P, G * 2 * D], U8, name="w2", align_bytes=64)
         w3 = sb.tile([P, G * 2 * D], U8, name="w3", align_bytes=64)
-        cb = sb.tile([P, 2 * NB], BF16, name="cb")
+        cb = sb.tile([P, NB], BF16, name="cb")
+        cb32 = sb.tile([P, NB], F32, name="cb32")
 
         def load_x(t):
             nc.sync.dma_start(out=xs[t][:], in_=x[t * P : (t + 1) * P, :])
@@ -84,17 +85,17 @@ def tile_three_residual_adapters_t2_kernel(
         load_w1(0)
         load_scales(0, 1, G)
         load_w1(1)
-        load_w1(2)
         load_x(2)
+        load_w1(2)
         load_x(3)
         load_scales(1, 0, G)
         load_w(1, w2)
         load_scales(2, 0, G)
         load_w(2, w3)
-        c_col = sb.tile([P, 2], F32, name="c_col")
+        c_col = sb.tile([P, 4], F32, name="c_col")
         with nc.allow_non_contiguous_dma(reason="one word of c to a partition"):
-            nc.sync.dma_start(out=c_col[:], in_=c[2 * NB :].bitcast(F32).rearrange("(i p) -> p i", p=P))
-        nc.sync.dma_start(out=cb[:], in_=c[: 2 * NB].partition_broadcast(P))
+            nc.sync.dma_start(out=c_col[:], in_=c[NB:].bitcast(F32).rearrange("(i p) -> p i", p=P))
+        nc.sync.dma_start(out=cb[:], in_=c[:NB].partition_broadcast(P))
 
         def weight(s, g, j):
             if s == 0:
@@ -189,21 +190,21 @@ def tile_three_residual_adapters_t2_kernel(
             nc.vector.tensor_tensor(out=resid[(1, t, j)], in0=acc[:], in1=resid[(2, t, j)], op=ALU.add)
 
         def scale_store(t, j):
-            if j < G - 1:
-                nc.gpsimd.tensor_tensor(
-                    out=resid[(2, t, j)], in0=resid[(1, t, j)], in1=cb[:, NB * j : NB * (j + 1)], op=ALU.mult
-                )
+            if j == 0:
+                nc.gpsimd.tensor_tensor(out=resid[(2, t, j)], in0=resid[(1, t, j)], in1=cb32[:], op=ALU.mult)
             else:
-                nc.vector.tensor_tensor(out=resid[(2, t, j)], in0=resid[(1, t, j)], in1=c_last[0], op=ALU.mult)
+                nc.vector.tensor_tensor(
+                    out=resid[(2, t, j)], in0=resid[(1, t, j)], in1=c_last[0][:, NB * (j - 1) : NB * j], op=ALU.mult
+                )
             nc.sync.dma_start(out=out[t * P : (t + 1) * P, NB * j : NB * (j + 1)], in_=resid[(2, t, j)])
 
         c_last = []
 
         def spread_c():
             bank = new_bank(keep=True)
-            for i in range(2):
+            for i in range(4):
                 nc.tensor.transpose(bank[:, i * P : (i + 1) * P], c_col[:, i : i + 1].to_broadcast([P, P]), ident[:])
-            c_last.append(bank[:, : 2 * P].bitcast(BF16))
+            c_last.append(bank[:].bitcast(BF16))
 
         def groups(s, t):
             return [(s, t, g) for g in range(G)]
@@ -266,8 +267,8 @@ def tile_three_residual_adapters_t2_kernel(
                     for item in to_quantise:
                         quantise(item)
                     to_quantise = []
-                if s == 2 and j < G - 1:
-                    scale_store(t, j)
+                if s == 2 and j != 1:
+                    scale_store(t, j // 2)
                 if s < 2:
                     late_cast.append((s, t, j))
                     if j < G - 1 or (s, t) not in runs:
@@ -285,6 +286,8 @@ def tile_three_residual_adapters_t2_kernel(
                 for stj in late_cast:
                     cast(*stj)
                 late_cast = []
+                if (s, t) == (1, 1):
+                    nc.scalar.copy(out=cb32[:], in_=cb[:])
                 for tj in late_mult:
                     scale_store(*tj)
                 late_mult = []

from contextlib import ExitStack

import concourse.mybir as mybir
from concourse.masks import make_identity

M, D = 512, 1536
FLOPS = 3 * 2 * M * D * D

F32 = mybir.dt.float32
BF16 = mybir.dt.bfloat16
I32 = mybir.dt.int32
U32 = mybir.dt.uint32
U8 = mybir.dt.uint8
FP8X4 = mybir.dt.float8_e4m3fn_x4
FP4X4 = mybir.dt.float4_e2m1fn_x4
ALU = mybir.AluOpType

P = 128
KP = 512
G = D // KP
NB = 512
TILES = M // P
BANKS = 8


def tile_three_residual_adapters_t2_kernel(
    tc, x, w1_words, w1_scales, w2_words, w2_scales, w3_words, w3_scales, c, out
):
    nc = tc.nc
    with ExitStack() as ctx:
        sb = ctx.enter_context(tc.tile_pool(name="sb", bufs=1))
        ps = ctx.enter_context(tc.psum_pool(name="ps", bufs=1))
        ctx.enter_context(tc.manual_schedule())

        used = []
        ring = list(range(BANKS))

        def new_bank(keep=False, back=None):
            n = len(used)
            used.append(n)
            b = ring.pop(0 if back is None else BANKS - back)
            if not keep:
                ring.append(b)
            return ps.tile([P, NB], F32, name="ps%d" % n, tag="bank%d" % b)

        words_in = [w1_words, w2_words, w3_words]
        scales_in = [w1_scales, w2_scales, w3_scales]
        planes = [sb.tile([P, G * D], U8, name="plane%d" % s, align_bytes=64) for s in range(3)]
        for s in range(3):
            nc.vector.memset(planes[s][:].bitcast(I32), 0)
        ident = sb.tile([P, P], F32, name="ident")
        make_identity(nc, ident[:])

        xs = [sb.tile([P, D], BF16, name="x%d" % t, align_bytes=64) for t in range(TILES)]
        w1 = [sb.tile([P, 2 * D], U8, name="w1_%d" % g, align_bytes=64) for g in range(G)]
        w2 = sb.tile([P, G * 2 * D], U8, name="w2", align_bytes=64)
        w3 = sb.tile([P, G * 2 * D], U8, name="w3", align_bytes=64)
        cb = sb.tile([P, NB], BF16, name="cb")
        cb32 = sb.tile([P, NB], F32, name="cb32")

        def load_x(t):
            nc.sync.dma_start(out=xs[t][:], in_=x[t * P : (t + 1) * P, :])

        def load_scales(s, g0, g1):
            src = scales_in[s].bitcast(I32).rearrange("g (q r) n -> r q g n", r=4)
            dst = planes[s][:].bitcast(I32)
            for r in range(4):
                nc.sync.dma_start(
                    out=dst[r:P:32, g0 * D // 4 : g1 * D // 4].rearrange("q (g n) -> q g n", g=g1 - g0),
                    in_=src[r][:, g0:g1, :],
                )

        def load_w1(g):
            nc.sync.dma_start(out=w1[g][:].bitcast(I32), in_=w1_words[g].bitcast(I32))

        def load_w(s, tile):
            nc.sync.dma_start(
                out=tile[:].bitcast(I32).rearrange("p (g n) -> p g n", g=G),
                in_=words_in[s].bitcast(I32).rearrange("g p n -> p g n"),
            )

        load_x(0)
        load_x(1)
        load_scales(0, 0, 1)
        load_w1(0)
        load_scales(0, 1, G)
        load_w1(1)
        load_x(2)
        load_w1(2)
        load_x(3)
        load_scales(1, 0, G)
        load_w(1, w2)
        load_scales(2, 0, G)
        load_w(2, w3)
        c_col = sb.tile([P, 4], F32, name="c_col")
        with nc.allow_non_contiguous_dma(reason="one word of c to a partition"):
            nc.sync.dma_start(out=c_col[:], in_=c[NB:].bitcast(F32).rearrange("(i p) -> p i", p=P))
        nc.sync.dma_start(out=cb[:], in_=c[:NB].partition_broadcast(P))

        def weight(s, g, j):
            if s == 0:
                wb = w1[g][:, 2 * NB * j : 2 * NB * (j + 1)]
            else:
                wb = (w2 if s == 1 else w3)[:, 2 * D * g + 2 * NB * j : 2 * D * g + 2 * NB * (j + 1)]
            return wb.bitcast(FP4X4), planes[s][:, D * g + NB * j : D * g + NB * (j + 1)]

        halves = {}
        quantised = {}
        resid = {}
        for t in range(TILES):
            for j in range(G):
                resid[(0, t, j)] = xs[t][:, NB * j : NB * (j + 1)]

        def x_direct(t):
            w = xs[t][:].bitcast(F32)
            for g in range(G):
                halves[(0, t, g)] = [w[:, 256 * g + u : 256 * (g + 1) : 2] for u in range(2)]

        def x_sorted(t):
            srt = sb.tile([P, D // 2], F32, name="xsort%d" % t)
            nc.vector.tensor_copy(
                out=srt[:].rearrange("p (g u m) -> p g u m", g=G, u=2),
                in_=xs[t][:].bitcast(F32).rearrange("p (g m u) -> p g u m", g=G, u=2),
            )
            for g in range(G):
                halves[(0, t, g)] = [srt[:, 256 * g + P * u : 256 * g + P * (u + 1)] for u in range(2)]

        def turn(chunks, back=None):
            done = []
            for keys in chunks:
                bank = new_bank(back=back)
                for i, key in enumerate(keys):
                    for u in range(2):
                        nc.tensor.transpose(bank[:, (2 * i + u) * P : (2 * i + u + 1) * P], halves[key][u], ident[:])
                done.append((keys, bank))
            return done

        def copy_out(item):
            keys, bank = item
            n = len(keys)
            label = "%d%d%d" % keys[0]
            grp = sb.tile([P, n * KP], BF16, name="grp" + label, align_bytes=64)
            nc.scalar.copy(
                out=grp[:].bitcast(F32).rearrange("p (i r u) -> p i r u", i=n, u=2),
                in_=bank[:, : n * 2 * P].rearrange("p (i u r) -> p i r u", i=n, u=2),
            )
            return keys, grp

        def quantise(item):
            keys, grp = item
            n = len(keys)
            label = "%d%d%d" % keys[0]
            codes = sb.tile([P, n * P], U32, name="codes" + label, align_bytes=64)
            scl = sb.tile([P, n * P], U8, name="scl" + label, align_bytes=64)
            nc.vector.quantize_mx(out=codes[:].bitcast(FP8X4), scales=scl[:], in_=grp[:])
            for i, key in enumerate(keys):
                quantised[key] = (codes[:, i * P : (i + 1) * P], scl[:, i * P : (i + 1) * P])

        def mm(acc, s, t, g, j):
            codes, scl = quantised[(s, t, g)]
            wb, ws = weight(s, g, j)
            nc.tensor.matmul_mx(
                out=acc[:], lhsT=codes.bitcast(FP8X4), lhsT_scale=scl, rhs=wb, rhs_scale=ws,
                start=(g == 0), stop=(g == G - 1),
            )

        def column(s, t, j):
            acc = new_bank()
            for g in range(G):
                mm(acc, s, t, g, j)
            return acc

        def add_relu(acc, s, t, j):
            h = sb.tile([P, NB], F32, name="h%d%d%d" % (s + 1, t, j))
            nc.vector.scalar_tensor_tensor(
                out=h[:], in0=acc[:], scalar=0.0, in1=resid[(s, t, j)], op0=ALU.max, op1=ALU.add
            )
            resid[(s + 1, t, j)] = h[:]

        def cast(s, t, j):
            hb = sb.tile([P, NB], BF16, name="hb%d%d%d" % (s + 1, t, j))
            nc.scalar.copy(
                out=hb[:].rearrange("p (u m e) -> p u m e", u=2, e=2),
                in_=resid[(s + 1, t, j)].rearrange("p (m u e) -> p u m e", u=2, e=2),
            )
            w = hb[:].bitcast(F32)
            halves[(s + 1, t, j)] = [w[:, P * u : P * (u + 1)] for u in range(2)]

        def add_last(acc, t, j):
            nc.vector.tensor_tensor(out=resid[(1, t, j)], in0=acc[:], in1=resid[(2, t, j)], op=ALU.add)

        def scale_store(t, j):
            if j == 0:
                nc.gpsimd.tensor_tensor(out=resid[(2, t, j)], in0=resid[(1, t, j)], in1=cb32[:], op=ALU.mult)
            else:
                nc.vector.tensor_tensor(
                    out=resid[(2, t, j)], in0=resid[(1, t, j)], in1=c_last[0][:, NB * (j - 1) : NB * j], op=ALU.mult
                )
            nc.sync.dma_start(out=out[t * P : (t + 1) * P, NB * j : NB * (j + 1)], in_=resid[(2, t, j)])

        c_last = []

        def spread_c():
            bank = new_bank(keep=True)
            for i in range(4):
                nc.tensor.transpose(bank[:, i * P : (i + 1) * P], c_col[:, i : i + 1].to_broadcast([P, P]), ident[:])
            c_last.append(bank[:].bitcast(BF16))

        def groups(s, t):
            return [(s, t, g) for g in range(G)]

        def in_twos(keys):
            return [keys[i : i + 2] for i in range(0, len(keys), 2)]

        x_direct(0)
        x_direct(1)
        for t in range(2):
            for item in [copy_out(i) for i in turn(in_twos(groups(0, t)))]:
                quantise(item)
        x_sorted(2)
        x_sorted(3)
        accs = {}
        for t in range(2):
            for j in range(G):
                accs[(t, j)] = new_bank()
        for g in range(G - 1):
            for t in range(2):
                for j in range(G):
                    mm(accs[(t, j)], 0, t, g, j)
        x2 = [copy_out(i) for i in turn(in_twos(groups(0, 2)))]
        for t in range(2):
            for j in range(G):
                mm(accs[(t, j)], 0, t, G - 1, j)
        turned = turn(in_twos(groups(0, 3)), back=2)
        for j in range(2):
            add_relu(accs[(0, j)], 0, 0, j)
            cast(0, 0, j)
        for item in x2:
            quantise(item)
        x3 = [copy_out(i) for i in turned]
        for t, j in [(0, 2), (1, 0), (1, 1), (1, 2)]:
            add_relu(accs[(t, j)], 0, t, j)
            cast(0, t, j)

        units = [(0, 2), (0, 3), (1, 0), (1, 1), (1, 2), (2, 0), (1, 3), (2, 1), (2, 2), (2, 3)]
        runs = {
            (0, 2): [(1, 0), (1, 1)],
            (1, 0): [(1, 2), (1, 3)],
            (1, 1): [(2, 0)],
            (2, 0): [(2, 1), (2, 2)],
            (2, 1): [(2, 3)],
        }
        to_quantise = x3
        late_cast = []
        late_mult = []
        for s, t in units:
            for j in range(G):
                acc = column(s, t, j)
                if s < 2:
                    add_relu(acc, s, t, j)
                else:
                    add_last(acc, t, j)
                if j == 0:
                    for tj in late_mult:
                        scale_store(*tj)
                    late_mult = []
                    for item in to_quantise:
                        quantise(item)
                    to_quantise = []
                if s == 2 and j != 1:
                    scale_store(t, j // 2)
                if s < 2:
                    late_cast.append((s, t, j))
                    if j < G - 1 or (s, t) not in runs:
                        for stj in late_cast:
                            cast(*stj)
                        late_cast = []
            if s == 2:
                late_mult = [(t, G - 1)]
            if (s, t) in runs:
                keys = [k for st in runs[(s, t)] for k in groups(*st)]
                turned = turn(in_twos(keys))
                if (s, t) == (1, 1):
                    spread_c()
                items = [copy_out(i) for i in turned]
                for stj in late_cast:
                    cast(*stj)
                late_cast = []
                if (s, t) == (1, 1):
                    nc.scalar.copy(out=cb32[:], in_=cb[:])
                for tj in late_mult:
                    scale_store(*tj)
                late_mult = []
                for item in items[:2]:
                    quantise(item)
                to_quantise = items[2:]
        for tj in late_mult:
            scale_store(*tj)
